import numpy as np
import ml_dtypes


def mxq(x, axis, fmt="e4m3"):
    dtype, down = {"e4m3": (ml_dtypes.float8_e4m3fn, 7), "e5m2": (ml_dtypes.float8_e5m2, 14)}[fmt]
    v = np.moveaxis(np.asarray(x, np.float32).astype(ml_dtypes.bfloat16).astype(np.float64), axis, -1)
    blocks = v.reshape(v.shape[:-1] + (-1, 32))
    amax = np.abs(blocks).max(-1, keepdims=True)
    byte = np.maximum(np.where(amax > 0, np.frexp(amax)[1] - 1 + 127, 0) - down, 1)
    scale = np.exp2(byte - 127.0)
    codes = (blocks / scale).astype(np.float32).astype(dtype).astype(np.float64)
    return np.moveaxis((codes * scale).reshape(v.shape), -1, axis)


WIDE = False


def mx_kscale(k):
    if not WIDE:
        return np.ones(k)
    levels = np.array([10, -10, 5, -5, 0])
    if k % 512:
        return np.exp2(np.random.permutation(np.resize(levels, k // 32))).repeat(32)
    a = np.empty((k // 512, 16))
    for p in range(k // 512):
        a[p, :8] = np.random.permutation(np.resize(levels, 8))
        for g in range(8):
            far = levels[np.abs(levels - a[p, g]) >= 10]
            a[p, g + 8] = far[np.random.randint(len(far))]
    return np.exp2(a.ravel()).repeat(32)


def f64(x):
    return np.asarray(x).astype(np.float64)


def striped(idx):
    return np.tile(np.asarray(idx).reshape(-1, 16).T, (8, 1)).astype(np.uint16)


def unstriped(offs):
    return offs[:16].T.reshape(-1).astype(np.int64)


E2M1 = np.array([0.0, 0.5, 1.0, 1.5, 2.0, 3.0, 4.0, 6.0, -0.0, -0.5, -1.0, -1.5, -2.0, -3.0, -4.0, -6.0])


def pack_weight(w, fmt):
    k, n = w.shape
    w = f64(np.asarray(w, np.float32).astype(ml_dtypes.bfloat16)).reshape(k // 32, 32, n)
    amax = np.abs(w).max(1)
    if fmt == "e4m3":
        byte = np.frexp(amax)[1] - 1 + 127 - 7
    else:
        mant, ex = np.frexp(amax / 6.0)
        byte = np.where(mant > 0.5, ex, ex - 1) + 127
    byte = np.clip(np.where(amax > 0, byte, 1), 1, 254)
    scaled = (w * np.exp2(127.0 - byte)[:, None, :]).reshape(k, n).astype(np.float32)
    by_word = np.ascontiguousarray(scaled.reshape(k // 512, 128, 4, n).transpose(0, 1, 3, 2))
    if fmt == "e4m3":
        words = by_word.astype(ml_dtypes.float8_e4m3fn).view(np.uint8)
    else:
        c = by_word.astype(ml_dtypes.float4_e2m1fn).view(np.uint8) & 0xF
        words = (c[..., 0::2] | (c[..., 1::2] << 4)).reshape(k // 512, 128, 2 * n)
    return np.ascontiguousarray(words), np.ascontiguousarray(byte.astype(np.uint8).reshape(k // 512, 16, n))


def unpack_weight(words, scales, fmt):
    g, _, n = scales.shape
    words = np.ascontiguousarray(words).reshape(g, 128, n, -1)
    if fmt == "e4m3":
        vals = words.view(ml_dtypes.float8_e4m3fn).astype(np.float64)
    else:
        nib = np.empty((g, 128, n, 4), np.uint8)
        nib[..., 0::2] = words & 0xF
        nib[..., 1::2] = words >> 4
        vals = E2M1[nib]
    vals = vals * np.repeat(np.exp2(scales.astype(np.float64) - 127.0), 8, axis=1)[..., None]
    return vals.transpose(0, 1, 3, 2).reshape(g * 512, n)


def softplus(v):
    return np.log(1.0 + np.exp(v))


def sigmoid(v):
    return 1.0 / (1.0 + np.exp(-v))


def bf(x):
    return np.asarray(x, np.float32).astype(ml_dtypes.bfloat16)


def planes(Y):
    r, m = Y.shape
    b = f64(bf(Y)).reshape(r // 32, 32, m)
    amax = np.abs(b).max(1)
    byte = np.clip(np.where(amax > 0, np.frexp(amax)[1] - 1 + 127 - 7, 1), 1, 254)
    codes = (b * np.exp2(127.0 - byte)[:, None, :]).reshape(r, m).astype(np.float32).astype(ml_dtypes.float8_e4m3fn).view(np.uint8)
    words = codes.reshape(r // 512, 128, 4, m).transpose(0, 1, 3, 2)
    return np.ascontiguousarray(words), np.ascontiguousarray(byte.astype(np.uint8).reshape(r // 512, 16, m))


K, R, F, T, J, M = 512, 512, 512, 2048, 512, 256


def setup_inputs():
    n = np.random.standard_normal
    idx = np.random.permutation(T)[:J]
    idx2 = np.random.permutation(J)[:M]
    idx3 = np.random.permutation(J)[:M]
    fk = mx_kscale(K)
    ff = mx_kscale(F)
    tabp = pack_weight(n((K, T)) / fk[:, None], "e4m3")
    return {
        "tab_words": tabp[0],
        "tab_scales": tabp[1],
        "w1": (n((K, R)) * 1 / np.sqrt(K) * fk[:, None]).astype(np.float32),
        "bias": (np.random.uniform(-0.5, 0.5, (R, 1))).astype(np.float32),
        "reserve": (np.random.uniform(0.3, 1.0, (R, 1))).astype(np.float32),
        "wo": (n((F, R)) * 1 / np.sqrt(F) * ff[:, None]).astype(np.float32),
        "dy": (n((F, M)) / ff[:, None]).astype(np.float32),
        "old": (0.5 * n((R, J))).astype(np.float32),
        "offs": striped(idx),
        "offs2": striped(idx2),
        "offs3": striped(idx3),
    }


def reference(tab_words, tab_scales, w1, bias, reserve, wo, dy, old, offs, offs2, offs3):
    idx = unstriped(offs)
    idx2 = unstriped(offs2)
    idx3 = unstriped(offs3)
    tabu = unpack_weight(tab_words, tab_scales, "e4m3")
    w1q = mxq(f64(w1), 0, "e4m3")
    tabidxg = tabu[:, idx]
    a = w1q.T @ tabidxg
    h1 = softplus(a + f64(bias))
    s = h1[:, idx2] * h1[:, idx3]
    woq = mxq(f64(wo), 0, "e4m3")
    dyq = mxq(f64(dy), 0, "e4m3")
    c0 = woq.T @ dyq
    ds = c0 / (s + h1[:, idx2] + f64(reserve)) - c0 * s / np.square(s + h1[:, idx2] + f64(reserve))
    e1 = c0 * s / np.square(s + h1[:, idx2] + f64(reserve)) * (-1.0)
    s1 = np.zeros((R, J))
    s1[:, idx2] = e1
    e2 = ds * h1[:, idx3]
    s2 = np.zeros((R, J))
    s2[:, idx2] = e2
    e3 = ds * h1[:, idx2]
    s3 = np.zeros((R, J))
    s3[:, idx3] = e3
    dh1 = s1 + s2 + s3
    da = dh1 * sigmoid(a + f64(bias))
    y = da + f64(old)
    words, scales = planes(y)
    return y, words, scales

@@ -1,0 +1,220 @@
+from contextlib import ExitStack
+
+import concourse.mybir as mybir
+from concourse.masks import make_identity
+
+FLOPS = 402653184
+
+F32 = mybir.dt.float32
+BF16 = mybir.dt.bfloat16
+I32 = mybir.dt.int32
+U32 = mybir.dt.uint32
+U16 = mybir.dt.uint16
+U8 = mybir.dt.uint8
+FP8X4 = mybir.dt.float8_e4m3fn_x4
+ALU = mybir.AluOpType
+ACT = mybir.ActivationFunctionType
+
+P = 128
+PACK = 4
+T, J, M = 2048, 512, 256
+R = 512
+TINY = 2.0 ** -62
+DEAL_SPLIT = 80
+
+
+def tile_attend_cpairshare_pl_kernel(tc, tab_words, tab_scales, w1, bias, reserve, wo, dy, old,
+                                      offs, offs2, offs3, out_0, out_1, out_2):
+    nc = tc.nc
+    with ExitStack() as ctx:
+        lists = ctx.enter_context(tc.tile_pool(name="lists", bufs=1))
+        sb = ctx.enter_context(tc.tile_pool(name="sb", bufs=1))
+        ps = ctx.enter_context(tc.psum_pool(name="ps", bufs=1))
+
+        def tile(name, shape, dtype):
+            return sb.tile(shape, dtype, name=name, align_bytes=64)
+
+        slots = lists.tile([P, J // 16], U16, name="slots")
+        nc.sync.dma_start(slots[:], offs)
+        w1_raw = tile("w1_raw", [P, PACK, R], F32)
+        nc.sync.dma_start(w1_raw[:], w1.rearrange("(p j) c -> p j c", j=PACK))
+        tab_sc = tile("tab_sc", [P, T], U8)
+        nc.vector.memset(tab_sc[:].bitcast(I32), 0)
+        for q in range(4):
+            nc.scalar.dma_start(tab_sc[32 * q : 32 * q + 4, :].bitcast(I32), tab_scales[0, 4 * q : 4 * q + 4, :].bitcast(I32))
+        tab_w = tile("tab_w", [P, T], U32)
+        nc.sync.dma_start(tab_w[:].bitcast(I32), tab_words[0].rearrange("p c t -> p (c t)").bitcast(I32))
+        bias_sb = tile("bias_sb", [P, PACK], F32)
+        nc.sync.dma_start(bias_sb[:], bias.rearrange("(p t) o -> p (t o)", t=PACK))
+        res_sb = tile("res_sb", [P, PACK], F32)
+        nc.sync.dma_start(res_sb[:], reserve.rearrange("(p t) o -> p (t o)", t=PACK))
+        wo_raw = tile("wo_raw", [P, PACK, R], F32)
+        nc.sync.dma_start(wo_raw[:], wo.rearrange("(p j) c -> p j c", j=PACK))
+        dy_raw = tile("dy_raw", [P, PACK, M], F32)
+        nc.sync.dma_start(dy_raw[:], dy.rearrange("(p j) c -> p j c", j=PACK))
+        first = lists.tile([P, M // 16], U16, name="first")
+        nc.sync.dma_start(first[:], offs2)
+        second = lists.tile([P, M // 16], U16, name="second")
+        nc.sync.dma_start(second[:], offs3)
+        old_sb = tile("old_sb", [P, PACK, J], F32)
+        nc.sync.dma_start(old_sb[:], old.rearrange("(p t) c -> p t c", t=PACK))
+
+        ident = tile("ident", [P, P], F32)
+        make_identity(nc, ident[:])
+
+        put2 = [tile(f"put2_{t}", [P, J], F32) for t in range(PACK)]
+        put3 = [tile(f"put3_{t}", [P, J], F32) for t in range(PACK)]
+        for window in put2 + put3:
+            nc.vector.memset(window[:], 0.0)
+
+        col_sc = tile("col_sc", [P, J], U8)
+        nc.vector.tensor_copy(col_sc[:], tab_sc[:].indirect(slots[:]))
+
+        def dealt(raw, name):
+            grouped = tile(name, [P, PACK, P, PACK], BF16)
+            return grouped, grouped[:].rearrange("p t m j -> p m t j"), raw[:].rearrange("p j (m t) -> p m t j", t=PACK)
+
+        def quantise(grouped_flat, width, name):
+            codes = tile(name + "_codes", [P, width], U32)
+            scales = tile(name + "_scales", [P, width], U8)
+            nc.vector.quantize_mx(codes[:].bitcast(FP8X4), scales[:], grouped_flat)
+            return codes, scales
+
+        w1_g, dst, src = dealt(w1_raw, "w1_g")
+        nc.vector.tensor_copy(dst[:, :DEAL_SPLIT], src[:, :DEAL_SPLIT])
+        nc.scalar.copy(dst[:, DEAL_SPLIT:], src[:, DEAL_SPLIT:])
+        w1_codes, w1_scales = quantise(w1_g[:].rearrange("p t m j -> p (t m j)"), R, "w1")
+
+        col_w = tile("col_w", [P, J], U32)
+        nc.vector.tensor_copy(col_w[:], tab_w[:].indirect(slots[:]))
+
+        neg_bias = tile("neg_bias", [P, PACK], F32)
+        nc.vector.tensor_scalar(neg_bias[:], bias_sb[:], -1.0, None, ALU.mult)
+
+        a_ps = [ps.tile([P, J], F32, name=f"a_ps{t}") for t in range(PACK)]
+        for t in range(PACK):
+            cols = slice(t * P, (t + 1) * P)
+            nc.tensor.matmul_mx(a_ps[t][:], lhsT=w1_codes[:, cols].bitcast(FP8X4), lhsT_scale=w1_scales[:, cols],
+                                rhs=col_w[:].bitcast(FP8X4), rhs_scale=col_sc[:], start=True, stop=True)
+        nsig = [tile(f"nsig{t}", [P, J], F32) for t in range(PACK)]
+        z = [tile(f"z{t}", [P, J], F32) for t in range(PACK)]
+        for t in range(PACK):
+            nc.scalar.activation(nsig[t][:], a_ps[t][:], ACT.Sigmoid, bias=neg_bias[:, t : t + 1], scale=-1.0)
+        for t in range(PACK):
+            nc.vector.tensor_scalar(z[t][:], a_ps[t][:], bias_sb[:, t : t + 1], None, ALU.add)
+
+        wo_g, dst, src = dealt(wo_raw, "wo_g")
+        nc.vector.tensor_copy(dst, src)
+        dy_g = tile("dy_g", [P, M, PACK], BF16)
+        nc.vector.tensor_copy(dy_g[:].rearrange("p (c i) j -> p c j i", i=4), dy_raw[:].rearrange("p j (c i) -> p c j i", i=4))
+        wo_codes, wo_scales = quantise(wo_g[:].rearrange("p t m j -> p (t m j)"), R, "wo")
+        dy_codes, dy_scales = quantise(dy_g[:].rearrange("p c j -> p (c j)"), M, "dy")
+        c_ps = [ps.tile([P, 2, M], F32, name=f"c_ps{g}") for g in range(2)]
+        for t in range(PACK):
+            cols = slice(t * P, (t + 1) * P)
+            nc.tensor.matmul_mx(c_ps[t // 2][:, t % 2, :], lhsT=wo_codes[:, cols].bitcast(FP8X4), lhsT_scale=wo_scales[:, cols],
+                                rhs=dy_codes[:].bitcast(FP8X4), rhs_scale=dy_scales[:], start=True, stop=True)
+
+        lns = [tile(f"lns{t}", [P, J], F32) for t in range(PACK)]
+        for t in range(PACK):
+            nc.scalar.activation(lns[t][:], nsig[t][:], ACT.Ln, bias=TINY)
+        h1 = [tile(f"h1_{t}", [P, J], F32) for t in range(PACK)]
+        expo = [tile(f"expo{g}", [P, 2, 3, M], F32) for g in range(2)]
+        decay = [tile(f"decay{g}", [P, 2, 3, M], F32) for g in range(2)]
+        den_sq = [tile(f"den_sq{g}", [P, 2, M], F32) for g in range(2)]
+        h3_res = [tile(f"h3_res{t}", [P, M], F32) for t in range(PACK)]
+        h2_w = [tile(f"h2_w{t}", [P, M], F32) for t in range(PACK)]
+
+        def softplus(t):
+            nc.vector.scalar_tensor_tensor(h1[t][:], lns[t][:], -1.0, z[t][:], ALU.mult, ALU.max)
+
+        def look_up(t, which):
+            nc.vector.tensor_copy(expo[t // 2][:, t % 2, which, :], h1[t][:].indirect((first, second)[which][:]))
+
+        def denominator(t):
+            res = res_sb[:, t : t + 1]
+            h2, h3 = expo[t // 2][:, t % 2, 0, :], expo[t // 2][:, t % 2, 1, :]
+            s_h2 = tile(f"s_h2_{t}", [P, M], F32)
+            nc.vector.scalar_tensor_tensor(s_h2[:], h3, 1.0, h2, ALU.add, ALU.mult)
+            nc.scalar.activation(den_sq[t // 2][:, t % 2, :], s_h2[:], ACT.Square, bias=res)
+            nc.scalar.activation(h3_res[t][:], h3, ACT.Copy, scale=res)
+
+        def numerator(t):
+            h2 = expo[t // 2][:, t % 2, 0, :]
+            nc.vector.scalar_tensor_tensor(h2_w[t][:], h2, res_sb[:, t : t + 1], h2, ALU.add, ALU.mult)
+
+        def decays(g):
+            nc.scalar.activation(expo[g][:, :, 2, :], den_sq[g][:], ACT.Ln)
+            for u in range(2):
+                nc.scalar.activation(decay[g][:, u], expo[g][:, u], ACT.Exp, scale=-1.0)
+
+        y = tile("y", [P, PACK, J], F32)
+        out_rows = out_0.rearrange("(p t) c -> p t c", t=PACK)
+
+        def put(t):
+            d = decay[t // 2][:, t % 2]
+            q = tile(f"q{t}", [P, M], F32)
+            f2 = tile(f"f2_{t}", [P, M], F32)
+            f3 = tile(f"f3_{t}", [P, M], F32)
+            nc.vector.scalar_tensor_tensor(q[:], c_ps[t // 2][:, t % 2, :], -1.0, d[:, 2, :], ALU.mult, ALU.mult)
+            nc.vector.scalar_tensor_tensor(f2[:], d[:, 0, :], 1.0, h3_res[t][:], ALU.subtract, ALU.mult)
+            nc.vector.scalar_tensor_tensor(f3[:], d[:, 1, :], 1.0, h2_w[t][:], ALU.subtract, ALU.mult)
+            nc.vector.tensor_tensor(put2[t][:].indirect(first[:]), q[:], f2[:], ALU.mult)
+            nc.vector.tensor_tensor(put3[t][:].indirect(second[:]), q[:], f3[:], ALU.mult)
+
+        def sum_on_tensor(terms, turned_ps, turned, back_ps):
+            for b in range(J // P):
+                cols = slice(b * P, (b + 1) * P)
+                for n, term in enumerate(terms):
+                    nc.tensor.matmul(turned_ps[:, cols], lhsT=term[:, cols], rhs=ident[:], is_transpose=True,
+                                     start=(n == 0), stop=(n == len(terms) - 1))
+            nc.scalar.copy(turned[:], turned_ps[:])
+            for b in range(J // P):
+                cols = slice(b * P, (b + 1) * P)
+                nc.tensor.transpose(back_ps[:, cols], turned[:, cols], ident[:])
+
+        softplus(0)
+        for t in range(PACK):
+            look_up(t, 0)
+            look_up(t, 1)
+            if t + 1 < PACK:
+                softplus(t + 1)
+            else:
+                numerator(t)
+            denominator(t)
+            if t + 1 < PACK:
+                numerator(t)
+            if t % 2:
+                decays(t // 2)
+        last = PACK - 1
+        for t in range(PACK):
+            put(t)
+            turned = tile(f"turned{t}", [P, J], F32)
+            turned_ps, back_ps = a_ps[2 * (t % 2)], a_ps[2 * (t % 2) + 1]
+            if t < last:
+                sum_on_tensor([old_sb[:, t, :], put2[t][:], put3[t][:]], turned_ps, turned, back_ps)
+                nc.scalar.copy(y[:, t, :], back_ps[:])
+                nc.sync.dma_start(out_rows[:, t, :], y[:, t, :])
+            else:
+                sum_on_tensor([old_sb[:, t, :], put2[t][:]], turned_ps, turned, back_ps)
+
+        y_g = tile("y_g", [P, J, PACK], BF16)
+        y_codes = tile("y_codes", [P, J], U32)
+        y_scales = tile("y_scales", [P, J], U8)
+        upper, low0, low1 = slice(256, 512), slice(0, 128), slice(128, 256)
+        for cols in (upper, low0, low1):
+            nc.vector.tensor_tensor(y[:, last, cols], back_ps[:, cols], put3[last][:, cols], ALU.add)
+        nc.sync.dma_start(out_rows[:, last, :], y[:, last, :])
+
+        def weave(copy, cols):
+            copy(y_g[:, cols, :].rearrange("p (c i) t -> p c t i", i=4), y[:, :, cols].rearrange("p t (c i) -> p c t i", i=4))
+
+        weave(nc.scalar.copy, upper)
+        weave(nc.vector.tensor_copy, low0)
+        weave(nc.vector.tensor_copy, low1)
+        for cols in (low0, low1, upper):
+            nc.vector.quantize_mx(y_codes[:, cols].bitcast(FP8X4), y_scales[:, cols], y_g[:, cols, :].rearrange("p c t -> p (c t)"))
+        nc.sync.dma_start(out_1[0].rearrange("p c t -> p (c t)").bitcast(I32), y_codes[:].bitcast(I32))
+        for q in range(4):
+            queue = nc.scalar if q % 2 else nc.sync
+            queue.dma_start(out_2[0, 4 * q : 4 * q + 4, :].bitcast(I32), y_scales[32 * q : 32 * q + 4, :].bitcast(I32))

@@ -21,6 +21,7 @@ T, J, M = 2048, 512, 256
 R = 512
 TINY = 2.0 ** -62
 DEAL_SPLIT = 80
+HALF = J // 2
 
 
 def tile_attend_cpairshare_pl_kernel(tc, tab_words, tab_scales, w1, bias, reserve, wo, dy, old,
@@ -39,9 +40,9 @@ def tile_attend_cpairshare_pl_kernel(tc, tab_words, tab_scales, w1, bias, reserv
         w1_raw = tile("w1_raw", [P, PACK, R], F32)
         nc.sync.dma_start(w1_raw[:], w1.rearrange("(p j) c -> p j c", j=PACK))
         tab_sc = tile("tab_sc", [P, T], U8)
-        nc.vector.memset(tab_sc[:].bitcast(I32), 0)
+        nc.gpsimd.memset(tab_sc[:].bitcast(I32), 0)
         for q in range(4):
-            nc.scalar.dma_start(tab_sc[32 * q : 32 * q + 4, :].bitcast(I32), tab_scales[0, 4 * q : 4 * q + 4, :].bitcast(I32))
+            nc.sync.dma_start(tab_sc[32 * q : 32 * q + 4, :].bitcast(I32), tab_scales[0, 4 * q : 4 * q + 4, :].bitcast(I32))
         tab_w = tile("tab_w", [P, T], U32)
         nc.sync.dma_start(tab_w[:].bitcast(I32), tab_words[0].rearrange("p c t -> p (c t)").bitcast(I32))
         bias_sb = tile("bias_sb", [P, PACK], F32)
@@ -64,8 +65,13 @@ def tile_attend_cpairshare_pl_kernel(tc, tab_words, tab_scales, w1, bias, reserv
 
         put2 = [tile(f"put2_{t}", [P, J], F32) for t in range(PACK)]
         put3 = [tile(f"put3_{t}", [P, J], F32) for t in range(PACK)]
-        for window in put2 + put3:
-            nc.vector.memset(window[:], 0.0)
+        for t in range(PACK):
+            engine = nc.gpsimd if t == PACK - 1 else nc.vector
+            engine.memset(put2[t][:], 0.0)
+            engine.memset(put3[t][:], 0.0)
+
+        warm = tile("warm", [P, 1], F32)
+        nc.scalar.activation(warm[:], ident[:, 0:1], ACT.Sigmoid)
 
         col_sc = tile("col_sc", [P, J], U8)
         nc.vector.tensor_copy(col_sc[:], tab_sc[:].indirect(slots[:]))
@@ -85,23 +91,26 @@ def tile_attend_cpairshare_pl_kernel(tc, tab_words, tab_scales, w1, bias, reserv
         nc.scalar.copy(dst[:, DEAL_SPLIT:], src[:, DEAL_SPLIT:])
         w1_codes, w1_scales = quantise(w1_g[:].rearrange("p t m j -> p (t m j)"), R, "w1")
 
-        col_w = tile("col_w", [P, J], U32)
-        nc.vector.tensor_copy(col_w[:], tab_w[:].indirect(slots[:]))
+        col_w = [tile(f"col_w{h}", [P, HALF], U32) for h in range(2)]
+        for h in range(2):
+            nc.vector.tensor_copy(col_w[h][:], tab_w[:].indirect(slots[:, h * HALF // 16 : (h + 1) * HALF // 16]))
 
         neg_bias = tile("neg_bias", [P, PACK], F32)
         nc.vector.tensor_scalar(neg_bias[:], bias_sb[:], -1.0, None, ALU.mult)
 
-        a_ps = [ps.tile([P, J], F32, name=f"a_ps{t}") for t in range(PACK)]
-        for t in range(PACK):
-            cols = slice(t * P, (t + 1) * P)
-            nc.tensor.matmul_mx(a_ps[t][:], lhsT=w1_codes[:, cols].bitcast(FP8X4), lhsT_scale=w1_scales[:, cols],
-                                rhs=col_w[:].bitcast(FP8X4), rhs_scale=col_sc[:], start=True, stop=True)
+        a_ps = [ps.tile([P, 2, HALF], F32, name=f"a_ps{n}") for n in range(4)]
+        pieces = [(h, t) for h in range(2) for t in range(PACK)]
         nsig = [tile(f"nsig{t}", [P, J], F32) for t in range(PACK)]
-        z = [tile(f"z{t}", [P, J], F32) for t in range(PACK)]
-        for t in range(PACK):
-            nc.scalar.activation(nsig[t][:], a_ps[t][:], ACT.Sigmoid, bias=neg_bias[:, t : t + 1], scale=-1.0)
-        for t in range(PACK):
-            nc.vector.tensor_scalar(z[t][:], a_ps[t][:], bias_sb[:, t : t + 1], None, ALU.add)
+        z0 = tile("z0", [P, J], F32)
+        for h, t in pieces:
+            cols = slice(t * P, (t + 1) * P)
+            nc.tensor.matmul_mx(a_ps[2 * h + t // 2][:, t % 2, :], lhsT=w1_codes[:, cols].bitcast(FP8X4), lhsT_scale=w1_scales[:, cols],
+                                rhs=col_w[h][:].bitcast(FP8X4), rhs_scale=col_sc[:, h * HALF : (h + 1) * HALF], start=True, stop=True)
+        for h, t in pieces:
+            nc.scalar.activation(nsig[t][:, h * HALF : (h + 1) * HALF], a_ps[2 * h + t // 2][:, t % 2, :], ACT.Sigmoid,
+                                 bias=neg_bias[:, t : t + 1], scale=-1.0)
+        for h in range(2):
+            nc.vector.tensor_scalar(z0[:, h * HALF : (h + 1) * HALF], a_ps[2 * h][:, 0, :], bias_sb[:, 0:1], None, ALU.add)
 
         wo_g, dst, src = dealt(wo_raw, "wo_g")
         nc.vector.tensor_copy(dst, src)
@@ -115,9 +124,12 @@ def tile_attend_cpairshare_pl_kernel(tc, tab_words, tab_scales, w1, bias, reserv
             nc.tensor.matmul_mx(c_ps[t // 2][:, t % 2, :], lhsT=wo_codes[:, cols].bitcast(FP8X4), lhsT_scale=wo_scales[:, cols],
                                 rhs=dy_codes[:].bitcast(FP8X4), rhs_scale=dy_scales[:], start=True, stop=True)
 
+        neg_lns = [tile(f"neg_lns{t}", [P, J], F32) if t > 0 else None for t in range(PACK)]
         lns = [tile(f"lns{t}", [P, J], F32) for t in range(PACK)]
         for t in range(PACK):
             nc.scalar.activation(lns[t][:], nsig[t][:], ACT.Ln, bias=TINY)
+            if t > 0:
+                nc.scalar.activation(neg_lns[t][:], lns[t][:], ACT.Copy, scale=-1.0)
         h1 = [tile(f"h1_{t}", [P, J], F32) for t in range(PACK)]
         expo = [tile(f"expo{g}", [P, 2, 3, M], F32) for g in range(2)]
         decay = [tile(f"decay{g}", [P, 2, 3, M], F32) for g in range(2)]
@@ -126,7 +138,13 @@ def tile_attend_cpairshare_pl_kernel(tc, tab_words, tab_scales, w1, bias, reserv
         h2_w = [tile(f"h2_w{t}", [P, M], F32) for t in range(PACK)]
 
         def softplus(t):
-            nc.vector.scalar_tensor_tensor(h1[t][:], lns[t][:], -1.0, z[t][:], ALU.mult, ALU.max)
+            if t == 0:
+                nc.vector.scalar_tensor_tensor(h1[t][:], lns[t][:], -1.0, z0[:], ALU.mult, ALU.max)
+                return
+            for h in range(2):
+                cols = slice(h * HALF, (h + 1) * HALF)
+                nc.vector.scalar_tensor_tensor(h1[t][:, cols], a_ps[2 * h + t // 2][:, t % 2, :], bias_sb[:, t : t + 1],
+                                               neg_lns[t][:, cols], ALU.add, ALU.max)
 
         def look_up(t, which):
             nc.vector.tensor_copy(expo[t // 2][:, t % 2, which, :], h1[t][:].indirect((first, second)[which][:]))
@@ -162,16 +180,21 @@ def tile_attend_cpairshare_pl_kernel(tc, tab_words, tab_scales, w1, bias, reserv
             nc.vector.tensor_tensor(put2[t][:].indirect(first[:]), q[:], f2[:], ALU.mult)
             nc.vector.tensor_tensor(put3[t][:].indirect(second[:]), q[:], f3[:], ALU.mult)
 
-        def sum_on_tensor(terms, turned_ps, turned, back_ps):
-            for b in range(J // P):
-                cols = slice(b * P, (b + 1) * P)
-                for n, term in enumerate(terms):
-                    nc.tensor.matmul(turned_ps[:, cols], lhsT=term[:, cols], rhs=ident[:], is_transpose=True,
-                                     start=(n == 0), stop=(n == len(terms) - 1))
+        def sum_on_tensor(t):
+            turned_ps = ps.tile([P, J], F32, name="turned_ps")
+            terms = [old_sb[:, t, :], put2[t][:], put3[t][:]]
+            blocks = [slice(b * P, (b + 1) * P) for b in range(J // P)]
+            passes = [(term, cols) for term in terms for cols in blocks]
+            for n, (term, cols) in enumerate(passes):
+                nc.tensor.matmul(turned_ps[:, cols], lhsT=term[:, cols], rhs=ident[:], is_transpose=True,
+                                 start=(n == 0), stop=(n == len(passes) - 1))
+            turned = tile("turned", [P, J], F32)
             nc.scalar.copy(turned[:], turned_ps[:])
-            for b in range(J // P):
-                cols = slice(b * P, (b + 1) * P)
+            back_ps = ps.tile([P, J], F32, name="back_ps")
+            for cols in blocks:
                 nc.tensor.transpose(back_ps[:, cols], turned[:, cols], ident[:])
+            nc.scalar.copy(y[:, t, :], back_ps[:])
+            nc.sync.dma_start(out_rows[:, t, :], y[:, t, :])
 
         softplus(0)
         for t in range(PACK):
@@ -189,21 +212,17 @@ def tile_attend_cpairshare_pl_kernel(tc, tab_words, tab_scales, w1, bias, reserv
         last = PACK - 1
         for t in range(PACK):
             put(t)
-            turned = tile(f"turned{t}", [P, J], F32)
-            turned_ps, back_ps = a_ps[2 * (t % 2)], a_ps[2 * (t % 2) + 1]
             if t < last:
-                sum_on_tensor([old_sb[:, t, :], put2[t][:], put3[t][:]], turned_ps, turned, back_ps)
-                nc.scalar.copy(y[:, t, :], back_ps[:])
-                nc.sync.dma_start(out_rows[:, t, :], y[:, t, :])
-            else:
-                sum_on_tensor([old_sb[:, t, :], put2[t][:]], turned_ps, turned, back_ps)
+                sum_on_tensor(t)
+        part = tile("part", [P, J], F32)
+        nc.vector.tensor_tensor(part[:], old_sb[:, last, :], put2[last][:], ALU.add)
 
         y_g = tile("y_g", [P, J, PACK], BF16)
         y_codes = tile("y_codes", [P, J], U32)
         y_scales = tile("y_scales", [P, J], U8)
         upper, low0, low1 = slice(256, 512), slice(0, 128), slice(128, 256)
         for cols in (upper, low0, low1):
-            nc.vector.tensor_tensor(y[:, last, cols], back_ps[:, cols], put3[last][:, cols], ALU.add)
+            nc.vector.tensor_tensor(y[:, last, cols], part[:, cols], put3[last][:, cols], ALU.add)
         nc.sync.dma_start(out_rows[:, last, :], y[:, last, :])
 
         def weave(copy, cols):
@@ -212,9 +231,11 @@ def tile_attend_cpairshare_pl_kernel(tc, tab_words, tab_scales, w1, bias, reserv
         weave(nc.scalar.copy, upper)
         weave(nc.vector.tensor_copy, low0)
         weave(nc.vector.tensor_copy, low1)
+        out_words = out_1[0].rearrange("p c t -> p (c t)").bitcast(I32)
         for cols in (low0, low1, upper):
             nc.vector.quantize_mx(y_codes[:, cols].bitcast(FP8X4), y_scales[:, cols], y_g[:, cols, :].rearrange("p c t -> p (c t)"))
-        nc.sync.dma_start(out_1[0].rearrange("p c t -> p (c t)").bitcast(I32), y_codes[:].bitcast(I32))
+        for cols in (slice(0, HALF), upper):
+            nc.sync.dma_start(out_words[:, cols], y_codes[:, cols].bitcast(I32))
         for q in range(4):
             queue = nc.scalar if q % 2 else nc.sync
             queue.dma_start(out_2[0, 4 * q : 4 * q + 4, :].bitcast(I32), y_scales[32 * q : 32 * q + 4, :].bitcast(I32))

@@ -32,8 +32,8 @@ def tile_attend_cpairshare_pl_kernel(tc, tab_words, tab_scales, w1, bias, reserv
         sb = ctx.enter_context(tc.tile_pool(name="sb", bufs=1))
         ps = ctx.enter_context(tc.psum_pool(name="ps", bufs=1))
 
-        def tile(name, shape, dtype):
-            return sb.tile(shape, dtype, name=name, align_bytes=64)
+        def tile(name, shape, dtype, tag=None):
+            return sb.tile(shape, dtype, name=name, tag=tag or name, align_bytes=64)
 
         slots = lists.tile([P, J // 16], U16, name="slots")
         nc.sync.dma_start(slots[:], offs)
@@ -133,8 +133,7 @@ def tile_attend_cpairshare_pl_kernel(tc, tab_words, tab_scales, w1, bias, reserv
         h1 = [tile(f"h1_{t}", [P, J], F32) for t in range(PACK)]
         expo = [tile(f"expo{g}", [P, 2, 3, M], F32) for g in range(2)]
         decay = [tile(f"decay{g}", [P, 2, 3, M], F32) for g in range(2)]
-        den_sq = [tile(f"den_sq{g}", [P, 2, M], F32) for g in range(2)]
-        h3_res = [tile(f"h3_res{t}", [P, M], F32) for t in range(PACK)]
+        side = {}
         h2_w = [tile(f"h2_w{t}", [P, M], F32) for t in range(PACK)]
 
         def softplus(t):
@@ -146,23 +145,26 @@ def tile_attend_cpairshare_pl_kernel(tc, tab_words, tab_scales, w1, bias, reserv
                 nc.vector.scalar_tensor_tensor(h1[t][:, cols], a_ps[2 * h + t // 2][:, t % 2, :], bias_sb[:, t : t + 1],
                                                neg_lns[t][:, cols], ALU.add, ALU.max)
 
-        def look_up(t, which):
-            nc.vector.tensor_copy(expo[t // 2][:, t % 2, which, :], h1[t][:].indirect((first, second)[which][:]))
+        def look_up(t):
+            for which, places in enumerate((first, second)):
+                nc.vector.tensor_copy(expo[t // 2][:, t % 2, which, :], h1[t][:].indirect(places[:]))
 
         def denominator(t):
             res = res_sb[:, t : t + 1]
             h2, h3 = expo[t // 2][:, t % 2, 0, :], expo[t // 2][:, t % 2, 1, :]
             s_h2 = tile(f"s_h2_{t}", [P, M], F32)
             nc.vector.scalar_tensor_tensor(s_h2[:], h3, 1.0, h2, ALU.add, ALU.mult)
-            nc.scalar.activation(den_sq[t // 2][:, t % 2, :], s_h2[:], ACT.Square, bias=res)
-            nc.scalar.activation(h3_res[t][:], h3, ACT.Copy, scale=res)
+            if t % 2 == 0:
+                side[t // 2] = tile(f"side{t // 2}", [P, 2, 2, M], F32, tag="expo0" if t else None)
+            nc.scalar.activation(side[t // 2][:, 0, t % 2, :], s_h2[:], ACT.Square, bias=res)
+            nc.scalar.activation(side[t // 2][:, 1, t % 2, :], h3, ACT.Copy, scale=res)
 
         def numerator(t):
             h2 = expo[t // 2][:, t % 2, 0, :]
             nc.vector.scalar_tensor_tensor(h2_w[t][:], h2, res_sb[:, t : t + 1], h2, ALU.add, ALU.mult)
 
         def decays(g):
-            nc.scalar.activation(expo[g][:, :, 2, :], den_sq[g][:], ACT.Ln)
+            nc.scalar.activation(expo[g][:, :, 2, :], side[g][:, 0], ACT.Ln)
             for u in range(2):
                 nc.scalar.activation(decay[g][:, u], expo[g][:, u], ACT.Exp, scale=-1.0)
 
@@ -175,7 +177,7 @@ def tile_attend_cpairshare_pl_kernel(tc, tab_words, tab_scales, w1, bias, reserv
             f2 = tile(f"f2_{t}", [P, M], F32)
             f3 = tile(f"f3_{t}", [P, M], F32)
             nc.vector.scalar_tensor_tensor(q[:], c_ps[t // 2][:, t % 2, :], -1.0, d[:, 2, :], ALU.mult, ALU.mult)
-            nc.vector.scalar_tensor_tensor(f2[:], d[:, 0, :], 1.0, h3_res[t][:], ALU.subtract, ALU.mult)
+            nc.vector.scalar_tensor_tensor(f2[:], d[:, 0, :], 1.0, side[t // 2][:, 1, t % 2, :], ALU.subtract, ALU.mult)
             nc.vector.scalar_tensor_tensor(f3[:], d[:, 1, :], 1.0, h2_w[t][:], ALU.subtract, ALU.mult)
             nc.vector.tensor_tensor(put2[t][:].indirect(first[:]), q[:], f2[:], ALU.mult)
             nc.vector.tensor_tensor(put3[t][:].indirect(second[:]), q[:], f3[:], ALU.mult)
@@ -188,7 +190,7 @@ def tile_attend_cpairshare_pl_kernel(tc, tab_words, tab_scales, w1, bias, reserv
             for n, (term, cols) in enumerate(passes):
                 nc.tensor.matmul(turned_ps[:, cols], lhsT=term[:, cols], rhs=ident[:], is_transpose=True,
                                  start=(n == 0), stop=(n == len(passes) - 1))
-            turned = tile("turned", [P, J], F32)
+            turned = tile(f"turned{t}", [P, J], F32, tag="expo1")
             nc.scalar.copy(turned[:], turned_ps[:])
             back_ps = ps.tile([P, J], F32, name="back_ps")
             for cols in blocks:
@@ -197,18 +199,23 @@ def tile_attend_cpairshare_pl_kernel(tc, tab_words, tab_scales, w1, bias, reserv
             nc.sync.dma_start(out_rows[:, t, :], y[:, t, :])
 
         softplus(0)
-        for t in range(PACK):
-            look_up(t, 0)
-            look_up(t, 1)
-            if t + 1 < PACK:
-                softplus(t + 1)
-            else:
-                numerator(t)
-            denominator(t)
-            if t + 1 < PACK:
-                numerator(t)
-            if t % 2:
-                decays(t // 2)
+        look_up(0)
+        softplus(1)
+        denominator(0)
+        look_up(1)
+        numerator(0)
+        denominator(1)
+        decays(0)
+        softplus(2)
+        numerator(1)
+        look_up(2)
+        softplus(3)
+        denominator(2)
+        look_up(3)
+        numerator(2)
+        denominator(3)
+        numerator(3)
+        decays(1)
         last = PACK - 1
         for t in range(PACK):
             put(t)

@@ -37,6 +37,8 @@ def tile_attend_cpairshare_pl_kernel(tc, tab_words, tab_scales, w1, bias, reserv
 
         slots = lists.tile([P, J // 16], U16, name="slots")
         nc.sync.dma_start(slots[:], offs)
+        bias_sb = tile("bias_sb", [P, PACK], F32)
+        nc.sync.dma_start(bias_sb[:], bias.rearrange("(p t) o -> p (t o)", t=PACK))
         w1_raw = tile("w1_raw", [P, PACK, R], F32)
         nc.sync.dma_start(w1_raw[:], w1.rearrange("(p j) c -> p j c", j=PACK))
         tab_sc = tile("tab_sc", [P, T], U8)
@@ -45,8 +47,6 @@ def tile_attend_cpairshare_pl_kernel(tc, tab_words, tab_scales, w1, bias, reserv
             nc.sync.dma_start(tab_sc[32 * q : 32 * q + 4, :].bitcast(I32), tab_scales[0, 4 * q : 4 * q + 4, :].bitcast(I32))
         tab_w = tile("tab_w", [P, T], U32)
         nc.sync.dma_start(tab_w[:].bitcast(I32), tab_words[0].rearrange("p c t -> p (c t)").bitcast(I32))
-        bias_sb = tile("bias_sb", [P, PACK], F32)
-        nc.sync.dma_start(bias_sb[:], bias.rearrange("(p t) o -> p (t o)", t=PACK))
         res_sb = tile("res_sb", [P, PACK], F32)
         nc.sync.dma_start(res_sb[:], reserve.rearrange("(p t) o -> p (t o)", t=PACK))
         wo_raw = tile("wo_raw", [P, PACK, R], F32)
@@ -98,19 +98,18 @@ def tile_attend_cpairshare_pl_kernel(tc, tab_words, tab_scales, w1, bias, reserv
         neg_bias = tile("neg_bias", [P, PACK], F32)
         nc.vector.tensor_scalar(neg_bias[:], bias_sb[:], -1.0, None, ALU.mult)
 
-        a_ps = [ps.tile([P, 2, HALF], F32, name=f"a_ps{n}") for n in range(4)]
-        pieces = [(h, t) for h in range(2) for t in range(PACK)]
+        a_ps = [ps.tile([P, J], F32, name=f"a_ps{t}") for t in range(PACK)]
+        halves = [slice(h * HALF, (h + 1) * HALF) for h in range(2)]
         nsig = [tile(f"nsig{t}", [P, J], F32) for t in range(PACK)]
         z0 = tile("z0", [P, J], F32)
-        for h, t in pieces:
-            cols = slice(t * P, (t + 1) * P)
-            nc.tensor.matmul_mx(a_ps[2 * h + t // 2][:, t % 2, :], lhsT=w1_codes[:, cols].bitcast(FP8X4), lhsT_scale=w1_scales[:, cols],
-                                rhs=col_w[h][:].bitcast(FP8X4), rhs_scale=col_sc[:, h * HALF : (h + 1) * HALF], start=True, stop=True)
-        for h, t in pieces:
-            nc.scalar.activation(nsig[t][:, h * HALF : (h + 1) * HALF], a_ps[2 * h + t // 2][:, t % 2, :], ACT.Sigmoid,
-                                 bias=neg_bias[:, t : t + 1], scale=-1.0)
-        for h in range(2):
-            nc.vector.tensor_scalar(z0[:, h * HALF : (h + 1) * HALF], a_ps[2 * h][:, 0, :], bias_sb[:, 0:1], None, ALU.add)
+        for h, cols in enumerate(halves):
+            for t in range(PACK):
+                rows = slice(t * P, (t + 1) * P)
+                nc.tensor.matmul_mx(a_ps[t][:, cols], lhsT=w1_codes[:, rows].bitcast(FP8X4), lhsT_scale=w1_scales[:, rows],
+                                    rhs=col_w[h][:].bitcast(FP8X4), rhs_scale=col_sc[:, cols], start=True, stop=True)
+            for t in range(PACK):
+                nc.scalar.activation(nsig[t][:, cols], a_ps[t][:, cols], ACT.Sigmoid, bias=neg_bias[:, t : t + 1], scale=-1.0)
+        nc.vector.tensor_scalar(z0[:], a_ps[0][:], bias_sb[:, 0:1], None, ALU.add)
 
         wo_g, dst, src = dealt(wo_raw, "wo_g")
         nc.vector.tensor_copy(dst, src)
@@ -126,10 +125,11 @@ def tile_attend_cpairshare_pl_kernel(tc, tab_words, tab_scales, w1, bias, reserv
 
         neg_lns = [tile(f"neg_lns{t}", [P, J], F32) if t > 0 else None for t in range(PACK)]
         lns = [tile(f"lns{t}", [P, J], F32) for t in range(PACK)]
-        for t in range(PACK):
+        for cols in halves:
+            nc.scalar.activation(lns[0][:, cols], nsig[0][:, cols], ACT.Ln, bias=TINY)
+        for t in range(1, PACK):
             nc.scalar.activation(lns[t][:], nsig[t][:], ACT.Ln, bias=TINY)
-            if t > 0:
-                nc.scalar.activation(neg_lns[t][:], lns[t][:], ACT.Copy, scale=-1.0)
+            nc.scalar.activation(neg_lns[t][:], lns[t][:], ACT.Copy, scale=-1.0)
         h1 = [tile(f"h1_{t}", [P, J], F32) for t in range(PACK)]
         expo = [tile(f"expo{g}", [P, 2, 3, M], F32) for g in range(2)]
         decay = [tile(f"decay{g}", [P, 2, 3, M], F32) for g in range(2)]
@@ -138,12 +138,10 @@ def tile_attend_cpairshare_pl_kernel(tc, tab_words, tab_scales, w1, bias, reserv
 
         def softplus(t):
             if t == 0:
-                nc.vector.scalar_tensor_tensor(h1[t][:], lns[t][:], -1.0, z0[:], ALU.mult, ALU.max)
+                for cols in halves:
+                    nc.vector.scalar_tensor_tensor(h1[t][:, cols], lns[t][:, cols], -1.0, z0[:, cols], ALU.mult, ALU.max)
                 return
-            for h in range(2):
-                cols = slice(h * HALF, (h + 1) * HALF)
-                nc.vector.scalar_tensor_tensor(h1[t][:, cols], a_ps[2 * h + t // 2][:, t % 2, :], bias_sb[:, t : t + 1],
-                                               neg_lns[t][:, cols], ALU.add, ALU.max)
+            nc.vector.scalar_tensor_tensor(h1[t][:], a_ps[t][:], bias_sb[:, t : t + 1], neg_lns[t][:], ALU.add, ALU.max)
 
         def look_up(t):
             for which, places in enumerate((first, second)):
@@ -222,7 +220,8 @@ def tile_attend_cpairshare_pl_kernel(tc, tab_words, tab_scales, w1, bias, reserv
             if t < last:
                 sum_on_tensor(t)
         part = tile("part", [P, J], F32)
-        nc.vector.tensor_tensor(part[:], old_sb[:, last, :], put2[last][:], ALU.add)
+        for cols in halves[::-1]:
+            nc.vector.tensor_tensor(part[:, cols], old_sb[:, last, cols], put2[last][:, cols], ALU.add)
 
         y_g = tile("y_g", [P, J, PACK], BF16)
         y_codes = tile("y_codes", [P, J], U32)

from contextlib import ExitStack

import concourse.mybir as mybir
from concourse.masks import make_identity

FLOPS = 402653184

F32 = mybir.dt.float32
BF16 = mybir.dt.bfloat16
I32 = mybir.dt.int32
U32 = mybir.dt.uint32
U16 = mybir.dt.uint16
U8 = mybir.dt.uint8
FP8X4 = mybir.dt.float8_e4m3fn_x4
ALU = mybir.AluOpType
ACT = mybir.ActivationFunctionType

P = 128
PACK = 4
T, J, M = 2048, 512, 256
R = 512
TINY = 2.0 ** -62
DEAL_SPLIT = 80
HALF = J // 2


def tile_attend_cpairshare_pl_kernel(tc, tab_words, tab_scales, w1, bias, reserve, wo, dy, old,
                                      offs, offs2, offs3, out_0, out_1, out_2):
    nc = tc.nc
    with ExitStack() as ctx:
        lists = ctx.enter_context(tc.tile_pool(name="lists", bufs=1))
        sb = ctx.enter_context(tc.tile_pool(name="sb", bufs=1))
        ps = ctx.enter_context(tc.psum_pool(name="ps", bufs=1))

        def tile(name, shape, dtype, tag=None):
            return sb.tile(shape, dtype, name=name, tag=tag or name, align_bytes=64)

        slots = lists.tile([P, J // 16], U16, name="slots")
        nc.sync.dma_start(slots[:], offs)
        bias_sb = tile("bias_sb", [P, PACK], F32)
        nc.sync.dma_start(bias_sb[:], bias.rearrange("(p t) o -> p (t o)", t=PACK))
        w1_raw = tile("w1_raw", [P, PACK, R], F32)
        nc.sync.dma_start(w1_raw[:], w1.rearrange("(p j) c -> p j c", j=PACK))
        tab_sc = tile("tab_sc", [P, T], U8)
        nc.gpsimd.memset(tab_sc[:].bitcast(I32), 0)
        for q in range(4):
            nc.sync.dma_start(tab_sc[32 * q : 32 * q + 4, :].bitcast(I32), tab_scales[0, 4 * q : 4 * q + 4, :].bitcast(I32))
        tab_w = tile("tab_w", [P, T], U32)
        nc.sync.dma_start(tab_w[:].bitcast(I32), tab_words[0].rearrange("p c t -> p (c t)").bitcast(I32))
        res_sb = tile("res_sb", [P, PACK], F32)
        nc.sync.dma_start(res_sb[:], reserve.rearrange("(p t) o -> p (t o)", t=PACK))
        wo_raw = tile("wo_raw", [P, PACK, R], F32)
        nc.sync.dma_start(wo_raw[:], wo.rearrange("(p j) c -> p j c", j=PACK))
        dy_raw = tile("dy_raw", [P, PACK, M], F32)
        nc.sync.dma_start(dy_raw[:], dy.rearrange("(p j) c -> p j c", j=PACK))
        first = lists.tile([P, M // 16], U16, name="first")
        nc.sync.dma_start(first[:], offs2)
        second = lists.tile([P, M // 16], U16, name="second")
        nc.sync.dma_start(second[:], offs3)
        old_sb = tile("old_sb", [P, PACK, J], F32)
        nc.sync.dma_start(old_sb[:], old.rearrange("(p t) c -> p t c", t=PACK))

        ident = tile("ident", [P, P], F32)
        make_identity(nc, ident[:])

        put2 = [tile(f"put2_{t}", [P, J], F32) for t in range(PACK)]
        put3 = [tile(f"put3_{t}", [P, J], F32) for t in range(PACK)]
        for t in range(PACK):
            engine = nc.gpsimd if t == PACK - 1 else nc.vector
            engine.memset(put2[t][:], 0.0)
            engine.memset(put3[t][:], 0.0)

        warm = tile("warm", [P, 1], F32)
        nc.scalar.activation(warm[:], ident[:, 0:1], ACT.Sigmoid)

        col_sc = tile("col_sc", [P, J], U8)
        nc.vector.tensor_copy(col_sc[:], tab_sc[:].indirect(slots[:]))

        def dealt(raw, name):
            grouped = tile(name, [P, PACK, P, PACK], BF16)
            return grouped, grouped[:].rearrange("p t m j -> p m t j"), raw[:].rearrange("p j (m t) -> p m t j", t=PACK)

        def quantise(grouped_flat, width, name):
            codes = tile(name + "_codes", [P, width], U32)
            scales = tile(name + "_scales", [P, width], U8)
            nc.vector.quantize_mx(codes[:].bitcast(FP8X4), scales[:], grouped_flat)
            return codes, scales

        w1_g, dst, src = dealt(w1_raw, "w1_g")
        nc.vector.tensor_copy(dst[:, :DEAL_SPLIT], src[:, :DEAL_SPLIT])
        nc.scalar.copy(dst[:, DEAL_SPLIT:], src[:, DEAL_SPLIT:])
        w1_codes, w1_scales = quantise(w1_g[:].rearrange("p t m j -> p (t m j)"), R, "w1")

        col_w = [tile(f"col_w{h}", [P, HALF], U32) for h in range(2)]
        for h in range(2):
            nc.vector.tensor_copy(col_w[h][:], tab_w[:].indirect(slots[:, h * HALF // 16 : (h + 1) * HALF // 16]))

        neg_bias = tile("neg_bias", [P, PACK], F32)
        nc.vector.tensor_scalar(neg_bias[:], bias_sb[:], -1.0, None, ALU.mult)

        a_ps = [ps.tile([P, J], F32, name=f"a_ps{t}") for t in range(PACK)]
        halves = [slice(h * HALF, (h + 1) * HALF) for h in range(2)]
        nsig = [tile(f"nsig{t}", [P, J], F32) for t in range(PACK)]
        z0 = tile("z0", [P, J], F32)
        for h, cols in enumerate(halves):
            for t in range(PACK):
                rows = slice(t * P, (t + 1) * P)
                nc.tensor.matmul_mx(a_ps[t][:, cols], lhsT=w1_codes[:, rows].bitcast(FP8X4), lhsT_scale=w1_scales[:, rows],
                                    rhs=col_w[h][:].bitcast(FP8X4), rhs_scale=col_sc[:, cols], start=True, stop=True)
            for t in range(PACK):
                nc.scalar.activation(nsig[t][:, cols], a_ps[t][:, cols], ACT.Sigmoid, bias=neg_bias[:, t : t + 1], scale=-1.0)
        nc.vector.tensor_scalar(z0[:], a_ps[0][:], bias_sb[:, 0:1], None, ALU.add)

        wo_g, dst, src = dealt(wo_raw, "wo_g")
        nc.vector.tensor_copy(dst, src)
        dy_g = tile("dy_g", [P, M, PACK], BF16)
        nc.vector.tensor_copy(dy_g[:].rearrange("p (c i) j -> p c j i", i=4), dy_raw[:].rearrange("p j (c i) -> p c j i", i=4))
        wo_codes, wo_scales = quantise(wo_g[:].rearrange("p t m j -> p (t m j)"), R, "wo")
        dy_codes, dy_scales = quantise(dy_g[:].rearrange("p c j -> p (c j)"), M, "dy")
        c_ps = [ps.tile([P, 2, M], F32, name=f"c_ps{g}") for g in range(2)]
        for t in range(PACK):
            cols = slice(t * P, (t + 1) * P)
            nc.tensor.matmul_mx(c_ps[t // 2][:, t % 2, :], lhsT=wo_codes[:, cols].bitcast(FP8X4), lhsT_scale=wo_scales[:, cols],
                                rhs=dy_codes[:].bitcast(FP8X4), rhs_scale=dy_scales[:], start=True, stop=True)

        neg_lns = [tile(f"neg_lns{t}", [P, J], F32) if t > 0 else None for t in range(PACK)]
        lns = [tile(f"lns{t}", [P, J], F32) for t in range(PACK)]
        for cols in halves:
            nc.scalar.activation(lns[0][:, cols], nsig[0][:, cols], ACT.Ln, bias=TINY)
        for t in range(1, PACK):
            nc.scalar.activation(lns[t][:], nsig[t][:], ACT.Ln, bias=TINY)
            nc.scalar.activation(neg_lns[t][:], lns[t][:], ACT.Copy, scale=-1.0)
        h1 = [tile(f"h1_{t}", [P, J], F32) for t in range(PACK)]
        expo = [tile(f"expo{g}", [P, 2, 3, M], F32) for g in range(2)]
        decay = [tile(f"decay{g}", [P, 2, 3, M], F32) for g in range(2)]
        side = {}
        h2_w = [tile(f"h2_w{t}", [P, M], F32) for t in range(PACK)]

        def softplus(t):
            if t == 0:
                for cols in halves:
                    nc.vector.scalar_tensor_tensor(h1[t][:, cols], lns[t][:, cols], -1.0, z0[:, cols], ALU.mult, ALU.max)
                return
            nc.vector.scalar_tensor_tensor(h1[t][:], a_ps[t][:], bias_sb[:, t : t + 1], neg_lns[t][:], ALU.add, ALU.max)

        def look_up(t):
            for which, places in enumerate((first, second)):
                nc.vector.tensor_copy(expo[t // 2][:, t % 2, which, :], h1[t][:].indirect(places[:]))

        def denominator(t):
            res = res_sb[:, t : t + 1]
            h2, h3 = expo[t // 2][:, t % 2, 0, :], expo[t // 2][:, t % 2, 1, :]
            s_h2 = tile(f"s_h2_{t}", [P, M], F32)
            nc.vector.scalar_tensor_tensor(s_h2[:], h3, 1.0, h2, ALU.add, ALU.mult)
            if t % 2 == 0:
                side[t // 2] = tile(f"side{t // 2}", [P, 2, 2, M], F32, tag="expo0" if t else None)
            nc.scalar.activation(side[t // 2][:, 0, t % 2, :], s_h2[:], ACT.Square, bias=res)
            nc.scalar.activation(side[t // 2][:, 1, t % 2, :], h3, ACT.Copy, scale=res)

        def numerator(t):
            h2 = expo[t // 2][:, t % 2, 0, :]
            nc.vector.scalar_tensor_tensor(h2_w[t][:], h2, res_sb[:, t : t + 1], h2, ALU.add, ALU.mult)

        def decays(g):
            nc.scalar.activation(expo[g][:, :, 2, :], side[g][:, 0], ACT.Ln)
            for u in range(2):
                nc.scalar.activation(decay[g][:, u], expo[g][:, u], ACT.Exp, scale=-1.0)

        y = tile("y", [P, PACK, J], F32)
        out_rows = out_0.rearrange("(p t) c -> p t c", t=PACK)

        def put(t):
            d = decay[t // 2][:, t % 2]
            q = tile(f"q{t}", [P, M], F32)
            f2 = tile(f"f2_{t}", [P, M], F32)
            f3 = tile(f"f3_{t}", [P, M], F32)
            nc.vector.scalar_tensor_tensor(q[:], c_ps[t // 2][:, t % 2, :], -1.0, d[:, 2, :], ALU.mult, ALU.mult)
            nc.vector.scalar_tensor_tensor(f2[:], d[:, 0, :], 1.0, side[t // 2][:, 1, t % 2, :], ALU.subtract, ALU.mult)
            nc.vector.scalar_tensor_tensor(f3[:], d[:, 1, :], 1.0, h2_w[t][:], ALU.subtract, ALU.mult)
            nc.vector.tensor_tensor(put2[t][:].indirect(first[:]), q[:], f2[:], ALU.mult)
            nc.vector.tensor_tensor(put3[t][:].indirect(second[:]), q[:], f3[:], ALU.mult)

        def sum_on_tensor(t):
            turned_ps = ps.tile([P, J], F32, name="turned_ps")
            terms = [old_sb[:, t, :], put2[t][:], put3[t][:]]
            blocks = [slice(b * P, (b + 1) * P) for b in range(J // P)]
            passes = [(term, cols) for term in terms for cols in blocks]
            for n, (term, cols) in enumerate(passes):
                nc.tensor.matmul(turned_ps[:, cols], lhsT=term[:, cols], rhs=ident[:], is_transpose=True,
                                 start=(n == 0), stop=(n == len(passes) - 1))
            turned = tile(f"turned{t}", [P, J], F32, tag="expo1")
            nc.scalar.copy(turned[:], turned_ps[:])
            back_ps = ps.tile([P, J], F32, name="back_ps")
            for cols in blocks:
                nc.tensor.transpose(back_ps[:, cols], turned[:, cols], ident[:])
            nc.scalar.copy(y[:, t, :], back_ps[:])
            nc.sync.dma_start(out_rows[:, t, :], y[:, t, :])

        softplus(0)
        look_up(0)
        softplus(1)
        denominator(0)
        look_up(1)
        numerator(0)
        denominator(1)
        decays(0)
        softplus(2)
        numerator(1)
        look_up(2)
        softplus(3)
        denominator(2)
        look_up(3)
        numerator(2)
        denominator(3)
        numerator(3)
        decays(1)
        last = PACK - 1
        for t in range(PACK):
            put(t)
            if t < last:
                sum_on_tensor(t)
        part = tile("part", [P, J], F32)
        for cols in halves[::-1]:
            nc.vector.tensor_tensor(part[:, cols], old_sb[:, last, cols], put2[last][:, cols], ALU.add)

        y_g = tile("y_g", [P, J, PACK], BF16)
        y_codes = tile("y_codes", [P, J], U32)
        y_scales = tile("y_scales", [P, J], U8)
        upper, low0, low1 = slice(256, 512), slice(0, 128), slice(128, 256)
        for cols in (upper, low0, low1):
            nc.vector.tensor_tensor(y[:, last, cols], part[:, cols], put3[last][:, cols], ALU.add)
        nc.sync.dma_start(out_rows[:, last, :], y[:, last, :])

        def weave(copy, cols):
            copy(y_g[:, cols, :].rearrange("p (c i) t -> p c t i", i=4), y[:, :, cols].rearrange("p t (c i) -> p c t i", i=4))

        weave(nc.scalar.copy, upper)
        weave(nc.vector.tensor_copy, low0)
        weave(nc.vector.tensor_copy, low1)
        out_words = out_1[0].rearrange("p c t -> p (c t)").bitcast(I32)
        for cols in (low0, low1, upper):
            nc.vector.quantize_mx(y_codes[:, cols].bitcast(FP8X4), y_scales[:, cols], y_g[:, cols, :].rearrange("p c t -> p (c t)"))
        for cols in (slice(0, HALF), upper):
            nc.sync.dma_start(out_words[:, cols], y_codes[:, cols].bitcast(I32))
        for q in range(4):
            queue = nc.scalar if q % 2 else nc.sync
            queue.dma_start(out_2[0, 4 * q : 4 * q + 4, :].bitcast(I32), y_scales[32 * q : 32 * q + 4, :].bitcast(I32))
